import numpy as np
import ml_dtypes


def mxq(x, axis, fmt="e4m3"):
    dtype, down = {"e4m3": (ml_dtypes.float8_e4m3fn, 7), "e5m2": (ml_dtypes.float8_e5m2, 14)}[fmt]
    v = np.moveaxis(np.asarray(x, np.float32).astype(ml_dtypes.bfloat16).astype(np.float64), axis, -1)
    blocks = v.reshape(v.shape[:-1] + (-1, 32))
    amax = np.abs(blocks).max(-1, keepdims=True)
    byte = np.maximum(np.where(amax > 0, np.frexp(amax)[1] - 1 + 127, 0) - down, 1)
    scale = np.exp2(byte - 127.0)
    codes = (blocks / scale).astype(np.float32).astype(dtype).astype(np.float64)
    return np.moveaxis((codes * scale).reshape(v.shape), -1, axis)


WIDE = False


def mx_kscale(k):
    if not WIDE:
        return np.ones(k)
    levels = np.array([30, -30])
    if k % 512:
        return np.exp2(np.random.permutation(np.resize(levels, k // 32))).repeat(32)
    a = np.empty((k // 512, 16))
    for p in range(k // 512):
        a[p, :8] = np.random.permutation(np.resize(levels, 8))
        for g in range(8):
            far = levels[np.abs(levels - a[p, g]) >= 10]
            a[p, g + 8] = far[np.random.randint(len(far))]
    return np.exp2(a.ravel()).repeat(32)


def f64(x):
    return np.asarray(x).astype(np.float64)


def striped(idx):
    return np.tile(np.asarray(idx).reshape(-1, 16).T, (8, 1)).astype(np.uint16)


def unstriped(offs):
    return offs[:16].T.reshape(-1).astype(np.int64)


E2M1 = np.array([0.0, 0.5, 1.0, 1.5, 2.0, 3.0, 4.0, 6.0, -0.0, -0.5, -1.0, -1.5, -2.0, -3.0, -4.0, -6.0])


def pack_weight(w, fmt):
    k, n = w.shape
    w = f64(np.asarray(w, np.float32).astype(ml_dtypes.bfloat16)).reshape(k // 32, 32, n)
    amax = np.abs(w).max(1)
    if fmt in ("e4m3", "e5m2"):
        byte = np.frexp(amax)[1] - 1 + 127 - (7 if fmt == "e4m3" else 14)
    else:
        mant, ex = np.frexp(amax / 6.0)
        byte = np.where(mant > 0.5, ex, ex - 1) + 127
    byte = np.clip(np.where(amax > 0, byte, 1), 1, 254)
    scaled = (w * np.exp2(127.0 - byte)[:, None, :]).reshape(k, n).astype(np.float32)
    by_word = np.ascontiguousarray(scaled.reshape(k // 512, 128, 4, n).transpose(0, 1, 3, 2))
    if fmt in ("e4m3", "e5m2"):
        words = by_word.astype(ml_dtypes.float8_e4m3fn if fmt == "e4m3" else ml_dtypes.float8_e5m2).view(np.uint8)
    else:
        c = by_word.astype(ml_dtypes.float4_e2m1fn).view(np.uint8) & 0xF
        words = (c[..., 0::2] | (c[..., 1::2] << 4)).reshape(k // 512, 128, 2 * n)
    return np.ascontiguousarray(words), np.ascontiguousarray(byte.astype(np.uint8).reshape(k // 512, 16, n))


def unpack_weight(words, scales, fmt):
    g, _, n = scales.shape
    words = np.ascontiguousarray(words).reshape(g, 128, n, -1)
    if fmt in ("e4m3", "e5m2"):
        vals = words.view(ml_dtypes.float8_e4m3fn if fmt == "e4m3" else ml_dtypes.float8_e5m2).astype(np.float64)
    else:
        nib = np.empty((g, 128, n, 4), np.uint8)
        nib[..., 0::2] = words & 0xF
        nib[..., 1::2] = words >> 4
        vals = E2M1[nib]
    vals = vals * np.repeat(np.exp2(scales.astype(np.float64) - 127.0), 8, axis=1)[..., None]
    return vals.transpose(0, 1, 3, 2).reshape(g * 512, n)


def sigmoid(v):
    return 1.0 / (1.0 + np.exp(-v))


def sgn(shape):
    return np.random.uniform(0.5, 2.0, shape) * np.where(np.random.standard_normal(shape) < 0, -1.0, 1.0)


K, T, J, R, V, C, O, N, S = 512, 1024, 256, 512, 1024, 512, 256, 256, 1024


def setup_inputs():
    n = np.random.standard_normal
    idx = np.random.permutation(V)[:R]
    idx2 = np.random.permutation(T)[:J]
    idx3 = np.random.permutation(C)[:J]
    idx4 = np.random.permutation(C)[:J]
    idx5 = np.random.permutation(C)[:O]
    idx6 = np.random.permutation(C)[:O]
    idx7 = np.random.permutation(S)[:N]
    fk = mx_kscale(K)
    fr = mx_kscale(R)
    xtp = pack_weight(n((K, T)) / fk[:, None], "e4m3")
    wtp = pack_weight(n((K, V)) * 1 / np.sqrt(K) * fk[:, None], "e2m1")
    w2p = pack_weight(n((K, R)) * 1 / np.sqrt(K) * fk[:, None], "e5m2")
    vsp = pack_weight(n((R, S)) * 1 / np.sqrt(R) / fr[:, None], "e5m2")
    return {
        "xt_words": xtp[0],
        "xt_scales": xtp[1],
        "wt_words": wtp[0],
        "wt_scales": wtp[1],
        "w2_words": w2p[0],
        "w2_scales": w2p[1],
        "sa": (np.random.uniform(0.5, 1.6, (R, 1)) * fr[:, None]).astype(np.float32),
        "sg": (sgn((R, 1))).astype(np.float32),
        "bg": (np.random.uniform(-2.0, 2.0, (R, 1))).astype(np.float32),
        "vs_words": vsp[0],
        "vs_scales": vsp[1],
        "offs": striped(idx),
        "offs2": striped(idx2),
        "offs3": striped(idx3),
        "offs4": striped(idx4),
        "offs5": striped(idx5),
        "offs6": striped(idx6),
        "offs7": striped(idx7),
    }


def reference(xt_words, xt_scales, wt_words, wt_scales, w2_words, w2_scales, sa, sg, bg, vs_words, vs_scales, offs, offs2, offs3, offs4, offs5, offs6, offs7):
    idx = unstriped(offs)
    idx2 = unstriped(offs2)
    idx3 = unstriped(offs3)
    idx4 = unstriped(offs4)
    idx5 = unstriped(offs5)
    idx6 = unstriped(offs6)
    idx7 = unstriped(offs7)
    xtu = unpack_weight(xt_words, xt_scales, "e4m3")
    wtu = unpack_weight(wt_words, wt_scales, "e2m1")
    w2u = unpack_weight(w2_words, w2_scales, "e5m2")
    vsu = unpack_weight(vs_words, vs_scales, "e5m2")
    wtidxg = wtu[:, idx]
    xtidx2g = xtu[:, idx2]
    a = wtidxg.T @ xtidx2g
    b = w2u.T @ xtidx2g
    pw = np.zeros((R, C))
    pw[:, idx3] = a
    pv = np.zeros((R, C))
    pv[:, idx4] = b
    pg = pw + pv
    hid = pg[:, idx5] * f64(sa) * sigmoid(pg[:, idx6] * f64(sg) + f64(bg))
    vsidx7g = vsu[:, idx7]
    hidq = mxq(hid, 0, "e4m3")
    y = vsidx7g.T @ hidq
    return y

@@ -1,0 +1,188 @@
+from contextlib import ExitStack
+
+import concourse.mybir as mybir
+
+K, T, J, R, V, C, O, N, S = 512, 1024, 256, 512, 1024, 512, 256, 256, 1024
+FLOPS = 2 * K * R * J * 2 + 2 * R * N * O
+
+F32 = mybir.dt.float32
+BF16 = mybir.dt.bfloat16
+I32 = mybir.dt.int32
+U32 = mybir.dt.uint32
+U16 = mybir.dt.uint16
+U8 = mybir.dt.uint8
+E4M3 = mybir.dt.float8_e4m3fn_x4
+E5M2 = mybir.dt.float8_e5m2_x4
+E2M1 = mybir.dt.float4_e2m1fn_x4
+ACT = mybir.ActivationFunctionType
+ALU = mybir.AluOpType
+
+P = 128
+PACK = 4
+HALF = O // 2
+
+
+def tile_list_gatedshared_storeleads_store_plain_kernel(
+    tc, xt_words, xt_scales, wt_words, wt_scales, w2_words, w2_scales, sa, sg, bg,
+    vs_words, vs_scales, offs, offs2, offs3, offs4, offs5, offs6, offs7, out,
+):
+    nc = tc.nc
+    with ExitStack() as ctx:
+        held = ctx.enter_context(tc.tile_pool(name="held", bufs=1))
+        psum = ctx.enter_context(tc.psum_pool(name="psum", bufs=1))
+
+        def load_list(src, name):
+            t = held.tile(list(src.shape), U16, name=name)
+            nc.sync.dma_start(t[:], src)
+            return t
+
+        def load_words(src, dtype, width, name, queue):
+            t = held.tile([P, width], dtype, name=name, align_bytes=64)
+            queue.dma_start(t[:].bitcast(I32), src.bitcast(I32))
+            return t
+
+        def clear_plane(width, name):
+            t = held.tile([P, width], U8, name=name, align_bytes=64)
+            nc.vector.memset(t[:].bitcast(I32), 0)
+            return t
+
+        def load_plane(t, src, queue):
+            for r in range(4):
+                queue.dma_start(t[r:P:32, :].bitcast(I32), src[0, r:16:4, :].bitcast(I32))
+
+        def load_rows(src, name):
+            t = held.tile([P, PACK], F32, name=name)
+            nc.sync.dma_start(t[:], src.rearrange("(p t) one -> p (t one)", t=PACK))
+            return t
+
+        xs = clear_plane(T, "xs")
+        w2s = clear_plane(R, "w2s")
+        ws = clear_plane(V, "ws")
+
+        l2 = load_list(offs2, "l2")
+        load_plane(xs, xt_scales, nc.sync)
+        xw = load_words(xt_words[0].rearrange("p n t -> p (n t)"), U32, T, "xw", nc.sync)
+        w2w = load_words(w2_words[0].rearrange("p n t -> p (n t)"), U32, R, "w2w", nc.sync)
+        load_plane(w2s, w2_scales, nc.sync)
+        l1 = load_list(offs, "l1")
+        ww = load_words(wt_words[0], U16, V, "ww", nc.sync)
+        l4 = load_list(offs4, "l4")
+        load_plane(ws, wt_scales, nc.sync)
+        l3 = load_list(offs3, "l3")
+        l7 = load_list(offs7, "l7")
+        vsw = load_words(vs_words[0].rearrange("p n t -> p (n t)"), U32, S, "vsw", nc.sync)
+        l5 = load_list(offs5, "l5")
+        l6 = load_list(offs6, "l6")
+        sa_t = load_rows(sa, "sa_t")
+        sg_t = load_rows(sg, "sg_t")
+        bg_t = load_rows(bg, "bg_t")
+        vss = clear_plane(S, "vss")
+        load_plane(vss, vs_scales, nc.sync)
+
+        def dealt(ap):
+            return ap.rearrange("p (t m) -> p m t", t=PACK)
+
+        def paired(ap):
+            return ap.rearrange("p (m t) -> p m t", t=PACK)
+
+        xg = held.tile([P, J], U32, name="xg", align_bytes=64)
+        xsg = held.tile([P, J], U8, name="xsg", align_bytes=64)
+        w2d = held.tile([P, R], U32, name="w2d", align_bytes=64)
+        w2sd = held.tile([P, R], U8, name="w2sd", align_bytes=64)
+        wg = held.tile([P, R], U16, name="wg", align_bytes=64)
+        wd = held.tile([P, R], U16, name="wd", align_bytes=64)
+        wsd = held.tile([P, R], U8, name="wsd", align_bytes=64)
+
+        nc.scalar.copy(dealt(w2d[:]), paired(w2w[:]))
+        nc.vector.tensor_copy(xg[:], xw[:].indirect(l2[:]))
+        nc.vector.tensor_copy(xsg[:], xs[:].indirect(l2[:]))
+        nc.vector.tensor_copy(dealt(w2sd[:]), paired(w2s[:]))
+        nc.vector.tensor_copy(wg[:], ww[:].indirect(l1[:]))
+        nc.vector.tensor_copy(dealt(wd[:]), paired(wg[:]))
+        nc.vector.tensor_copy(dealt(wsd[:]), ws[:].indirect(l1[:]))
+
+        pw = [held.tile([P, C], F32, name="pw%d" % u) for u in range(2)]
+        pv = [held.tile([P, C], F32, name="pv%d" % t) for t in range(PACK)]
+        pg = [held.tile([P, C], F32, name="pg%d" % t) for t in range(PACK)]
+        for page in pv + pw:
+            nc.vector.memset(page[:], 0.0)
+
+        def products(words, scales, fmt, ts, name, copy, tag=None):
+            acc = psum.tile([P, len(ts), J], F32, name=name + "_ps")
+            for u, t in enumerate(ts):
+                cols = slice(t * P, (t + 1) * P)
+                nc.tensor.matmul_mx(
+                    out=acc[:, u, :], lhsT=words[:, cols].bitcast(fmt), lhsT_scale=scales[:, cols],
+                    rhs=xg[:].bitcast(E4M3), rhs_scale=xsg[:], start=True, stop=True,
+                )
+            res = held.tile([P, len(ts), J], F32, name=name, tag=tag or name, align_bytes=64)
+            copy(res[:], acc[:])
+            return [res[:, u, :] for u in range(len(ts))]
+
+        lin = held.tile([P, PACK, O], F32, name="lin")
+        gate = held.tile([P, PACK, O], F32, name="gate")
+
+        def put_b(t, b):
+            nc.scalar.activation(out=pv[t][:].indirect(l4[:]), in_=b, func=ACT.Copy)
+
+        def put_a(t, a, adder):
+            nc.vector.tensor_copy(pw[t % 2][:].indirect(l3[:]), a)
+            adder.tensor_tensor(pg[t][:], pw[t % 2][:], pv[t][:], ALU.add)
+
+        def fetch(t, lo, hi):
+            nc.scalar.activation(
+                out=lin[:, t, lo:hi], in_=pg[t][:].indirect(l5[:, lo // 16 : hi // 16]),
+                func=ACT.Copy, scale=sa_t[:, t : t + 1],
+            )
+            nc.scalar.activation(
+                out=gate[:, t, lo:hi], in_=pg[t][:].indirect(l6[:, lo // 16 : hi // 16]),
+                func=ACT.Sigmoid, scale=sg_t[:, t : t + 1], bias=bg_t[:, t : t + 1],
+            )
+
+        vg = held.tile([P, N], U32, name="vg", align_bytes=64)
+
+        (b0,) = products(w2d, w2sd, E5M2, [0], "b0", nc.scalar.copy)
+        (b1,) = products(w2d, w2sd, E5M2, [1], "b1", nc.scalar.copy)
+        put_b(0, b0)
+        b2, b3 = products(w2d, w2sd, E5M2, [2, 3], "b23", nc.scalar.copy)
+        put_b(1, b1)
+        put_b(2, b2)
+        put_b(3, b3)
+        nc.vector.tensor_copy(vg[:], vsw[:].indirect(l7[:]))
+        a0, a1 = products(wd, wsd, E2M1, [0, 1], "a01", nc.vector.tensor_copy)
+        put_a(0, a0, nc.gpsimd)
+        a2, a3 = products(wd, wsd, E2M1, [2, 3], "a23", nc.vector.tensor_copy)
+        put_a(1, a1, nc.gpsimd)
+        put_a(2, a2, nc.gpsimd)
+        put_a(3, a3, nc.vector)
+        fetch(0, 0, O)
+        fetch(1, 0, O)
+        fetch(2, 0, O)
+        fetch(3, 0, HALF)
+        fetch(3, HALF, O)
+
+        vsg = held.tile([P, N], U8, name="vsg", tag="a23", align_bytes=64)
+        nc.vector.tensor_copy(vsg[:], vss[:].indirect(l7[:]))
+
+        for h in range(2):
+            cols = slice(h * HALF, (h + 1) * HALF)
+            hid = held.tile([P, HALF * PACK], BF16, name="hid%d" % h, align_bytes=64)
+            nc.vector.tensor_tensor(
+                hid[:].rearrange("p (c i t) -> p c t i", i=4, t=PACK),
+                lin[:, :, cols].rearrange("p t (c i) -> p c t i", i=4),
+                gate[:, :, cols].rearrange("p t (c i) -> p c t i", i=4),
+                ALU.mult,
+            )
+            hq = held.tile([P, HALF], U32, name="hq%d" % h, align_bytes=64)
+            hs = held.tile([P, HALF], U8, name="hs%d" % h, align_bytes=64)
+            nc.vector.quantize_mx(out=hq[:].bitcast(E4M3), scales=hs[:], in_=hid[:])
+            y = psum.tile([P, 2, HALF], F32, name="y%d" % h)
+            for g in range(2):
+                rows = slice(g * P, (g + 1) * P)
+                nc.tensor.matmul_mx(
+                    out=y[:, g, :], lhsT=vg[:, rows].bitcast(E5M2), lhsT_scale=vsg[:, rows],
+                    rhs=hq[:].bitcast(E4M3), rhs_scale=hs[:], start=True, stop=True,
+                )
+            res = held.tile([P, 2, HALF], F32, name="res%d" % h)
+            nc.scalar.copy(res[:], y[:])
+            nc.sync.dma_start(out[:, cols].rearrange("(g p) o -> p g o", p=P), res[:])

@@ -41,9 +41,9 @@ def tile_list_gatedshared_storeleads_store_plain_kernel(
             queue.dma_start(t[:].bitcast(I32), src.bitcast(I32))
             return t
 
-        def clear_plane(width, name):
+        def clear_plane(width, name, engine):
             t = held.tile([P, width], U8, name=name, align_bytes=64)
-            nc.vector.memset(t[:].bitcast(I32), 0)
+            engine.memset(t[:].bitcast(I32), 0)
             return t
 
         def load_plane(t, src, queue):
@@ -55,28 +55,34 @@ def tile_list_gatedshared_storeleads_store_plain_kernel(
             nc.sync.dma_start(t[:], src.rearrange("(p t) one -> p (t one)", t=PACK))
             return t
 
-        xs = clear_plane(T, "xs")
-        w2s = clear_plane(R, "w2s")
-        ws = clear_plane(V, "ws")
+        xs = clear_plane(T, "xs", nc.gpsimd)
+        warm = held.tile([P, 1], F32, name="warm")
+        nc.gpsimd.memset(warm[:], 0.0)
+        warm_out = held.tile([P, 1], F32, name="warm_out")
+        nc.scalar.activation(out=warm_out[:], in_=warm[:], func=ACT.Sigmoid)
 
+        w2s = clear_plane(R, "w2s", nc.vector)
+        ws = clear_plane(V, "ws", nc.vector)
+
+        w2s_rows = held.tile([4, 4, R // 4], I32, name="w2s_rows")
+        nc.sync.dma_start(w2s_rows[:], w2_scales[0].bitcast(I32).rearrange("(q r) c -> r q c", r=4))
         l2 = load_list(offs2, "l2")
-        load_plane(xs, xt_scales, nc.sync)
         xw = load_words(xt_words[0].rearrange("p n t -> p (n t)"), U32, T, "xw", nc.sync)
         w2w = load_words(w2_words[0].rearrange("p n t -> p (n t)"), U32, R, "w2w", nc.sync)
-        load_plane(w2s, w2_scales, nc.sync)
+        load_plane(xs, xt_scales, nc.sync)
         l1 = load_list(offs, "l1")
         ww = load_words(wt_words[0], U16, V, "ww", nc.sync)
         l4 = load_list(offs4, "l4")
         load_plane(ws, wt_scales, nc.sync)
-        l3 = load_list(offs3, "l3")
-        l7 = load_list(offs7, "l7")
         vsw = load_words(vs_words[0].rearrange("p n t -> p (n t)"), U32, S, "vsw", nc.sync)
-        l5 = load_list(offs5, "l5")
         l6 = load_list(offs6, "l6")
-        sa_t = load_rows(sa, "sa_t")
         sg_t = load_rows(sg, "sg_t")
         bg_t = load_rows(bg, "bg_t")
-        vss = clear_plane(S, "vss")
+        l5 = load_list(offs5, "l5")
+        sa_t = load_rows(sa, "sa_t")
+        l7 = load_list(offs7, "l7")
+        l3 = load_list(offs3, "l3")
+        vss = clear_plane(S, "vss", nc.vector)
         load_plane(vss, vs_scales, nc.sync)
 
         def dealt(ap):
@@ -94,30 +100,38 @@ def tile_list_gatedshared_storeleads_store_plain_kernel(
         wsd = held.tile([P, R], U8, name="wsd", align_bytes=64)
 
         nc.scalar.copy(dealt(w2d[:]), paired(w2w[:]))
+        for q in range(4):
+            nc.vector.tensor_copy(w2s[32 * q : 32 * q + 4, :].bitcast(I32), w2s_rows[:, q, :])
+        nc.vector.tensor_copy(dealt(w2sd[:]), paired(w2s[:]))
         nc.vector.tensor_copy(xg[:], xw[:].indirect(l2[:]))
         nc.vector.tensor_copy(xsg[:], xs[:].indirect(l2[:]))
-        nc.vector.tensor_copy(dealt(w2sd[:]), paired(w2s[:]))
         nc.vector.tensor_copy(wg[:], ww[:].indirect(l1[:]))
-        nc.vector.tensor_copy(dealt(wd[:]), paired(wg[:]))
         nc.vector.tensor_copy(dealt(wsd[:]), ws[:].indirect(l1[:]))
+        nc.vector.tensor_copy(dealt(wd[:]), paired(wg[:]))
 
-        pw = [held.tile([P, C], F32, name="pw%d" % u) for u in range(2)]
-        pv = [held.tile([P, C], F32, name="pv%d" % t) for t in range(PACK)]
-        pg = [held.tile([P, C], F32, name="pg%d" % t) for t in range(PACK)]
-        for page in pv + pw:
+        pw = [held.tile([P, C], F32, name="pw%d" % u, align_bytes=64) for u in range(2)]
+        pv = [held.tile([P, C], F32, name="pv%d" % t, align_bytes=64) for t in range(PACK)]
+        pg = [held.tile([P, C], F32, name="pg%d" % t, align_bytes=64) for t in range(2)]
+        for page in (pv[0], pv[1], pv[2]):
             nc.vector.memset(page[:], 0.0)
+        for page in (pw[0], pv[3], pw[1]):
+            nc.gpsimd.memset(page[:], 0.0)
 
-        def products(words, scales, fmt, ts, name, copy, tag=None):
-            acc = psum.tile([P, len(ts), J], F32, name=name + "_ps")
-            for u, t in enumerate(ts):
+        of_a = (wd, wsd, E2M1)
+        of_b = (w2d, w2sd, E5M2)
+
+        def products(parts, name, copy, res=None):
+            acc = psum.tile([P, len(parts), J], F32, name=name + "_ps")
+            for u, ((words, scales, fmt), t) in enumerate(parts):
                 cols = slice(t * P, (t + 1) * P)
                 nc.tensor.matmul_mx(
                     out=acc[:, u, :], lhsT=words[:, cols].bitcast(fmt), lhsT_scale=scales[:, cols],
                     rhs=xg[:].bitcast(E4M3), rhs_scale=xsg[:], start=True, stop=True,
                 )
-            res = held.tile([P, len(ts), J], F32, name=name, tag=tag or name, align_bytes=64)
-            copy(res[:], acc[:])
-            return [res[:, u, :] for u in range(len(ts))]
+            if res is None:
+                res = held.tile([P, len(parts), J], F32, name=name)[:]
+            copy(res, acc[:])
+            return [res[:, u, :] for u in range(len(parts))]
 
         lin = held.tile([P, PACK, O], F32, name="lin")
         gate = held.tile([P, PACK, O], F32, name="gate")
@@ -139,34 +153,37 @@ def tile_list_gatedshared_storeleads_store_plain_kernel(
                 func=ACT.Sigmoid, scale=sg_t[:, t : t + 1], bias=bg_t[:, t : t + 1],
             )
 
-        vg = held.tile([P, N], U32, name="vg", align_bytes=64)
-
-        (b0,) = products(w2d, w2sd, E5M2, [0], "b0", nc.scalar.copy)
-        (b1,) = products(w2d, w2sd, E5M2, [1], "b1", nc.scalar.copy)
+        (b0,) = products([(of_b, 0)], "b0", nc.scalar.copy)
+        (b1,) = products([(of_b, 1)], "b1", nc.scalar.copy)
         put_b(0, b0)
-        b2, b3 = products(w2d, w2sd, E5M2, [2, 3], "b23", nc.scalar.copy)
+        (b2,) = products([(of_b, 2)], "b2", nc.scalar.copy)
         put_b(1, b1)
+        vg = held.tile([P, N], U32, name="vg", align_bytes=64)
+        nc.vector.tensor_copy(vg[:], vsw[:].indirect(l7[:]))
+        a012 = held.tile([P, 3, J], F32, name="a012", tag="vsw", align_bytes=64)
+        (a0,) = products([(of_a, 0)], "a0", nc.vector.tensor_copy, a012[:, 0:1, :])
+        a1, a2 = products([(of_a, 1), (of_a, 2)], "a12", nc.vector.tensor_copy, a012[:, 1:3, :])
+        b3, a3 = products([(of_b, 3), (of_a, 3)], "b3a3", nc.scalar.copy)
         put_b(2, b2)
         put_b(3, b3)
-        nc.vector.tensor_copy(vg[:], vsw[:].indirect(l7[:]))
-        a0, a1 = products(wd, wsd, E2M1, [0, 1], "a01", nc.vector.tensor_copy)
         put_a(0, a0, nc.gpsimd)
-        a2, a3 = products(wd, wsd, E2M1, [2, 3], "a23", nc.vector.tensor_copy)
         put_a(1, a1, nc.gpsimd)
-        put_a(2, a2, nc.gpsimd)
-        put_a(3, a3, nc.vector)
         fetch(0, 0, O)
+        pg.append(held.tile([P, C], F32, name="pg2", align_bytes=64))
+        put_a(2, a2, nc.gpsimd)
+        pg.append(held.tile([P, C], F32, name="pg3", tag="pv2", align_bytes=64))
+        put_a(3, a3, nc.vector)
         fetch(1, 0, O)
         fetch(2, 0, O)
         fetch(3, 0, HALF)
         fetch(3, HALF, O)
 
-        vsg = held.tile([P, N], U8, name="vsg", tag="a23", align_bytes=64)
+        vsg = held.tile([P, N], U8, name="vsg", tag="pv3", align_bytes=64)
         nc.vector.tensor_copy(vsg[:], vss[:].indirect(l7[:]))
 
         for h in range(2):
             cols = slice(h * HALF, (h + 1) * HALF)
-            hid = held.tile([P, HALF * PACK], BF16, name="hid%d" % h, align_bytes=64)
+            hid = held.tile([P, HALF * PACK], BF16, name="hid%d" % h, tag=("vss", "hid1")[h], align_bytes=64)
             nc.vector.tensor_tensor(
                 hid[:].rearrange("p (c i t) -> p c t i", i=4, t=PACK),
                 lin[:, :, cols].rearrange("p t (c i) -> p c t i", i=4),

from contextlib import ExitStack

import concourse.mybir as mybir

K, T, J, R, V, C, O, N, S = 512, 1024, 256, 512, 1024, 512, 256, 256, 1024
FLOPS = 2 * K * R * J * 2 + 2 * R * N * O

F32 = mybir.dt.float32
BF16 = mybir.dt.bfloat16
I32 = mybir.dt.int32
U32 = mybir.dt.uint32
U16 = mybir.dt.uint16
U8 = mybir.dt.uint8
E4M3 = mybir.dt.float8_e4m3fn_x4
E5M2 = mybir.dt.float8_e5m2_x4
E2M1 = mybir.dt.float4_e2m1fn_x4
ACT = mybir.ActivationFunctionType
ALU = mybir.AluOpType

P = 128
PACK = 4
HALF = O // 2


def tile_list_gatedshared_storeleads_store_plain_kernel(
    tc, xt_words, xt_scales, wt_words, wt_scales, w2_words, w2_scales, sa, sg, bg,
    vs_words, vs_scales, offs, offs2, offs3, offs4, offs5, offs6, offs7, out,
):
    nc = tc.nc
    with ExitStack() as ctx:
        held = ctx.enter_context(tc.tile_pool(name="held", bufs=1))
        psum = ctx.enter_context(tc.psum_pool(name="psum", bufs=1))

        def load_list(src, name):
            t = held.tile(list(src.shape), U16, name=name)
            nc.sync.dma_start(t[:], src)
            return t

        def load_words(src, dtype, width, name, queue):
            t = held.tile([P, width], dtype, name=name, align_bytes=64)
            queue.dma_start(t[:].bitcast(I32), src.bitcast(I32))
            return t

        def clear_plane(width, name, engine):
            t = held.tile([P, width], U8, name=name, align_bytes=64)
            engine.memset(t[:].bitcast(I32), 0)
            return t

        def load_plane(t, src, queue):
            for r in range(4):
                queue.dma_start(t[r:P:32, :].bitcast(I32), src[0, r:16:4, :].bitcast(I32))

        def load_rows(src, name):
            t = held.tile([P, PACK], F32, name=name)
            nc.sync.dma_start(t[:], src.rearrange("(p t) one -> p (t one)", t=PACK))
            return t

        xs = clear_plane(T, "xs", nc.gpsimd)
        warm = held.tile([P, 1], F32, name="warm")
        nc.gpsimd.memset(warm[:], 0.0)
        warm_out = held.tile([P, 1], F32, name="warm_out")
        nc.scalar.activation(out=warm_out[:], in_=warm[:], func=ACT.Sigmoid)

        w2s = clear_plane(R, "w2s", nc.vector)
        ws = clear_plane(V, "ws", nc.vector)

        w2s_rows = held.tile([4, 4, R // 4], I32, name="w2s_rows")
        nc.sync.dma_start(w2s_rows[:], w2_scales[0].bitcast(I32).rearrange("(q r) c -> r q c", r=4))
        l2 = load_list(offs2, "l2")
        xw = load_words(xt_words[0].rearrange("p n t -> p (n t)"), U32, T, "xw", nc.sync)
        w2w = load_words(w2_words[0].rearrange("p n t -> p (n t)"), U32, R, "w2w", nc.sync)
        load_plane(xs, xt_scales, nc.sync)
        l1 = load_list(offs, "l1")
        ww = load_words(wt_words[0], U16, V, "ww", nc.sync)
        l4 = load_list(offs4, "l4")
        load_plane(ws, wt_scales, nc.sync)
        vsw = load_words(vs_words[0].rearrange("p n t -> p (n t)"), U32, S, "vsw", nc.sync)
        l6 = load_list(offs6, "l6")
        sg_t = load_rows(sg, "sg_t")
        bg_t = load_rows(bg, "bg_t")
        l5 = load_list(offs5, "l5")
        sa_t = load_rows(sa, "sa_t")
        l7 = load_list(offs7, "l7")
        l3 = load_list(offs3, "l3")
        vss = clear_plane(S, "vss", nc.vector)
        load_plane(vss, vs_scales, nc.sync)

        def dealt(ap):
            return ap.rearrange("p (t m) -> p m t", t=PACK)

        def paired(ap):
            return ap.rearrange("p (m t) -> p m t", t=PACK)

        xg = held.tile([P, J], U32, name="xg", align_bytes=64)
        xsg = held.tile([P, J], U8, name="xsg", align_bytes=64)
        w2d = held.tile([P, R], U32, name="w2d", align_bytes=64)
        w2sd = held.tile([P, R], U8, name="w2sd", align_bytes=64)
        wg = held.tile([P, R], U16, name="wg", align_bytes=64)
        wd = held.tile([P, R], U16, name="wd", align_bytes=64)
        wsd = held.tile([P, R], U8, name="wsd", align_bytes=64)

        nc.scalar.copy(dealt(w2d[:]), paired(w2w[:]))
        for q in range(4):
            nc.vector.tensor_copy(w2s[32 * q : 32 * q + 4, :].bitcast(I32), w2s_rows[:, q, :])
        nc.vector.tensor_copy(dealt(w2sd[:]), paired(w2s[:]))
        nc.vector.tensor_copy(xg[:], xw[:].indirect(l2[:]))
        nc.vector.tensor_copy(xsg[:], xs[:].indirect(l2[:]))
        nc.vector.tensor_copy(wg[:], ww[:].indirect(l1[:]))
        nc.vector.tensor_copy(dealt(wsd[:]), ws[:].indirect(l1[:]))
        nc.vector.tensor_copy(dealt(wd[:]), paired(wg[:]))

        pw = [held.tile([P, C], F32, name="pw%d" % u, align_bytes=64) for u in range(2)]
        pv = [held.tile([P, C], F32, name="pv%d" % t, align_bytes=64) for t in range(PACK)]
        pg = [held.tile([P, C], F32, name="pg%d" % t, align_bytes=64) for t in range(2)]
        for page in (pv[0], pv[1], pv[2]):
            nc.vector.memset(page[:], 0.0)
        for page in (pw[0], pv[3], pw[1]):
            nc.gpsimd.memset(page[:], 0.0)

        of_a = (wd, wsd, E2M1)
        of_b = (w2d, w2sd, E5M2)

        def products(parts, name, copy, res=None):
            acc = psum.tile([P, len(parts), J], F32, name=name + "_ps")
            for u, ((words, scales, fmt), t) in enumerate(parts):
                cols = slice(t * P, (t + 1) * P)
                nc.tensor.matmul_mx(
                    out=acc[:, u, :], lhsT=words[:, cols].bitcast(fmt), lhsT_scale=scales[:, cols],
                    rhs=xg[:].bitcast(E4M3), rhs_scale=xsg[:], start=True, stop=True,
                )
            if res is None:
                res = held.tile([P, len(parts), J], F32, name=name)[:]
            copy(res, acc[:])
            return [res[:, u, :] for u in range(len(parts))]

        lin = held.tile([P, PACK, O], F32, name="lin")
        gate = held.tile([P, PACK, O], F32, name="gate")

        def put_b(t, b):
            nc.scalar.activation(out=pv[t][:].indirect(l4[:]), in_=b, func=ACT.Copy)

        def put_a(t, a, adder):
            nc.vector.tensor_copy(pw[t % 2][:].indirect(l3[:]), a)
            adder.tensor_tensor(pg[t][:], pw[t % 2][:], pv[t][:], ALU.add)

        def fetch(t, lo, hi):
            nc.scalar.activation(
                out=lin[:, t, lo:hi], in_=pg[t][:].indirect(l5[:, lo // 16 : hi // 16]),
                func=ACT.Copy, scale=sa_t[:, t : t + 1],
            )
            nc.scalar.activation(
                out=gate[:, t, lo:hi], in_=pg[t][:].indirect(l6[:, lo // 16 : hi // 16]),
                func=ACT.Sigmoid, scale=sg_t[:, t : t + 1], bias=bg_t[:, t : t + 1],
            )

        (b0,) = products([(of_b, 0)], "b0", nc.scalar.copy)
        (b1,) = products([(of_b, 1)], "b1", nc.scalar.copy)
        put_b(0, b0)
        (b2,) = products([(of_b, 2)], "b2", nc.scalar.copy)
        put_b(1, b1)
        vg = held.tile([P, N], U32, name="vg", align_bytes=64)
        nc.vector.tensor_copy(vg[:], vsw[:].indirect(l7[:]))
        a012 = held.tile([P, 3, J], F32, name="a012", tag="vsw", align_bytes=64)
        (a0,) = products([(of_a, 0)], "a0", nc.vector.tensor_copy, a012[:, 0:1, :])
        a1, a2 = products([(of_a, 1), (of_a, 2)], "a12", nc.vector.tensor_copy, a012[:, 1:3, :])
        b3, a3 = products([(of_b, 3), (of_a, 3)], "b3a3", nc.scalar.copy)
        put_b(2, b2)
        put_b(3, b3)
        put_a(0, a0, nc.gpsimd)
        put_a(1, a1, nc.gpsimd)
        fetch(0, 0, O)
        pg.append(held.tile([P, C], F32, name="pg2", align_bytes=64))
        put_a(2, a2, nc.gpsimd)
        pg.append(held.tile([P, C], F32, name="pg3", tag="pv2", align_bytes=64))
        put_a(3, a3, nc.vector)
        fetch(1, 0, O)
        fetch(2, 0, O)
        fetch(3, 0, HALF)
        fetch(3, HALF, O)

        vsg = held.tile([P, N], U8, name="vsg", tag="pv3", align_bytes=64)
        nc.vector.tensor_copy(vsg[:], vss[:].indirect(l7[:]))

        for h in range(2):
            cols = slice(h * HALF, (h + 1) * HALF)
            hid = held.tile([P, HALF * PACK], BF16, name="hid%d" % h, tag=("vss", "hid1")[h], align_bytes=64)
            nc.vector.tensor_tensor(
                hid[:].rearrange("p (c i t) -> p c t i", i=4, t=PACK),
                lin[:, :, cols].rearrange("p t (c i) -> p c t i", i=4),
                gate[:, :, cols].rearrange("p t (c i) -> p c t i", i=4),
                ALU.mult,
            )
            hq = held.tile([P, HALF], U32, name="hq%d" % h, align_bytes=64)
            hs = held.tile([P, HALF], U8, name="hs%d" % h, align_bytes=64)
            nc.vector.quantize_mx(out=hq[:].bitcast(E4M3), scales=hs[:], in_=hid[:])
            y = psum.tile([P, 2, HALF], F32, name="y%d" % h)
            for g in range(2):
                rows = slice(g * P, (g + 1) * P)
                nc.tensor.matmul_mx(
                    out=y[:, g, :], lhsT=vg[:, rows].bitcast(E5M2), lhsT_scale=vsg[:, rows],
                    rhs=hq[:].bitcast(E4M3), rhs_scale=hs[:], start=True, stop=True,
                )
            res = held.tile([P, 2, HALF], F32, name="res%d" % h)
            nc.scalar.copy(res[:], y[:])
            nc.sync.dma_start(out[:, cols].rearrange("(g p) o -> p g o", p=P), res[:])
